import numpy as np, ml_dtypes
CORES = [65,73,81,89,97,105,113,121]
N = 8
GR, GC, TK = 2, 4, 256
RA = [[2,2],[-2,2]]
CB = [[-1,-2,-1,2],[-2,-2,-2,1],[1,2,-1,-1],[-2,1,1,-1]]
def setup_inputs(rng):
    return {"x": rng.standard_normal((N, 128, TK), dtype=np.float32).astype(ml_dtypes.bfloat16), "a": (rng.standard_normal((N, 128, 128), dtype=np.float32) / 11).astype(ml_dtypes.bfloat16)}
def setup_inputs_big(rng):
    d = setup_inputs(rng)
    for k in ("x", "a"): d[k] = (d[k].astype(np.float32) * 1024.0).astype(d[k].dtype)
    return d
def setup_inputs_small(rng):
    d = setup_inputs(rng)
    for k in ("x", "a"): d[k] = (d[k].astype(np.float32) * (1 / 1024.0)).astype(d[k].dtype)
    return d
def setup_inputs_apart(rng):
    d = setup_inputs(rng)
    f = (10.0 ** rng.permutation(np.linspace(-1.5, 1.5, N))).astype(np.float32).reshape(N, 1, 1)
    for k in ("x", "a"): d[k] = (d[k].astype(np.float32) * f).astype(d[k].dtype)
    return d
def reference(x, a):
    X, A = x.astype(np.float64), a.astype(np.float64)
    y = np.zeros((N, 128, TK))
    for i in range(GR):
        for j in range(GC):
            t = sum(RA[i][k] * CB[j][l] * X[k * GC + l] for k in range(GR) for l in range(GC))
            y[i * GC + j] = A[i * GC + j].T @ t
    return {"y": y.astype(ml_dtypes.bfloat16)}

from concourse.bass import DstId, RemoteDMATransfer
from concourse.mybir import AluOpType

P = 128
W = 256
NR = 8
N_HAND = 8
N_PASS = 8
N_DIRECT = 8
PER_DIE = 1

SCRATCH = {
    "xd": ("dram", [P, W], "bfloat16"),
    "xs": ("sbuf", [P, W], "bfloat16"),
    "land": ("sbuf", [P, NR * W], "bfloat16"),
    "a0": ("sbuf", [P, P], "bfloat16"),
    "kc": ("sbuf", [P, NR * P], "bfloat16"),
    "ac": ("sbuf", [P, NR * P], "bfloat16"),
    "ps": ("psum", [P, W], "float32"),
    "ys": ("sbuf", [P, W], "bfloat16"),
}
SEMAPHORES = ["ldd", "lda", "ldx", "kset", "ascl", "hand", "sent", "mm", "cp", "st"] + ["arr%d" % s for s in range(NR)]


def _bits(mask):
    return [e for e in range(mask.bit_length()) if (mask >> e) & 1]


def _engines(topo, src, dsts, count, avoid=()):
    m = topo.mask(src, dsts[0])
    for d in dsts[1:]:
        m &= topo.mask(src, d)
    return [e for e in _bits(m) if e not in avoid][:count]


def _plan(T, topo):
    n = len(T.cores)
    plan = []
    for s, src in enumerate(T.cores):
        others = [T.cores[(s + d) % n] for d in range(1, n)]
        direct = [d for d in others if topo.may_write(src, d)]
        cross = [d for d in others if not topo.may_write(src, d)]
        cross.sort(key=lambda d: not topo.mates(topo.chip(src), topo.chip(d)))
        able = [h for h in range(topo.CHIPS * topo.CORES_PER_CHIP)
                if topo.chip(h) == topo.chip(src) and T.rank_of(h) is None
                and all(topo.may_write(h, d) for d in cross)]
        relays = []
        for q in sorted({topo.die(h) for h in able}, key=lambda q: q != topo.die(src)):
            relays += [h for h in able if topo.die(h) == q][:PER_DIE]
        share = -(-len(cross) // len(relays)) if cross else 0
        jobs = [(h, cross[i * share:(i + 1) * share]) for i, h in enumerate(relays)]
        plan.append((direct, [(h, ds) for h, ds in jobs if ds]))
    return plan


def _send(g, topo, dsts, engines, src_ap, dst_ap, remote_sem, local_sem):
    mask = 0
    for e in engines:
        mask |= 1 << e
    where = []
    for d in dsts:
        rid, pid, _ring = topo.addr(d)
        where.append(DstId(rid=rid, pnc=pid))
    g.remote_dma_fused(
        [RemoteDMATransfer(dst_ids=where, dma_engine_mask=mask, remote_sem=remote_sem,
                           srcs=[src_ap], dsts=[dst_ap] * len(dsts), alu_op=0)],
        local_sem=local_sem)


def rank_program(g, core, T, topo):
    S = T.sem
    plan = _plan(T, topo)
    rank = T.rank_of(core)

    if rank is None:
        for s, (_direct, jobs) in enumerate(plan):
            for h, dsts in jobs:
                if h != core:
                    continue
                eng = _engines(topo, core, dsts, N_PASS)
                g.wait_ge(S.hand, N_HAND)
                _send(g, topo, dsts, eng, T.xd[:], T.land[:, s * W:(s + 1) * W], S["arr%d" % s], S.sent)
                g.wait_ge(S.sent, len(eng))
        return

    RA, CB = T.tables["RA"], T.tables["CB"]
    gc = len(CB)
    coef = [RA[rank // gc][s // gc] * CB[rank % gc][s % gc] for s in range(len(T.cores))]
    kinds = sorted(set(coef))
    direct, jobs = plan[rank]

    g.sync.dma_start(T.xd[:], T.x[:]).then_inc(S.ldd, 16)
    g.sync.dma_start(T.a0[:], T.a[:]).then_inc(S.lda, 16)
    g.sync.dma_start(T.xs[:], T.x[:]).then_inc(S.ldx, 16)

    slot = T.land[:, rank * W:(rank + 1) * W]
    sent = 0
    g.wait_ge(S.ldd, 16)
    off = _engines(topo, core, direct, N_DIRECT) if direct else []
    if jobs:
        relays = [h for h, _ds in jobs]
        eng = _engines(topo, core, relays, N_HAND, avoid=off)
        if len(eng) < N_HAND:
            eng = _engines(topo, core, relays, N_HAND)
        _send(g, topo, relays, eng, T.xd[:], T.xd[:], S.hand, S.sent)
        sent += len(eng)
    if direct:
        _send(g, topo, direct, off, T.xd[:], slot, S["arr%d" % rank], S.sent)
        sent += len(off)

    for q, c in enumerate(kinds):
        g.vector.memset(T.kc[:, q * P:(q + 1) * P], float(c)).then_inc(S.kset, 1)
    g.vector.wait_ge(S.kset, len(kinds))
    g.vector.wait_ge(S.lda, 16)
    for q in range(len(kinds)):
        g.vector.tensor_tensor(T.ac[:, q * P:(q + 1) * P], T.a0[:], T.kc[:, q * P:(q + 1) * P],
                               AluOpType.mult).then_inc(S.ascl, 1)

    due = []
    for s, (s_direct, s_jobs) in enumerate(plan):
        if core in s_direct:
            due.append((0, 0, s, N_DIRECT))
        for r, (_h, ds) in enumerate(s_jobs):
            if core in ds:
                due.append((1 + ds.index(core), r, s, N_PASS))
    due.sort()

    def scaled(s):
        q = kinds.index(coef[s])
        return T.ac[:, q * P:(q + 1) * P]

    g.tensor.wait_ge(S.ascl, len(kinds))
    g.tensor.wait_ge(S.ldx, 16)
    g.tensor.matmul(T.ps[:], scaled(rank), T.xs[:], start=True, stop=not due).then_inc(S.mm, 1)
    for t, (_late, _r, s, count) in enumerate(due):
        g.tensor.wait_ge(S["arr%d" % s], count)
        g.tensor.matmul(T.ps[:], scaled(s), T.land[:, s * W:(s + 1) * W],
                        start=False, stop=t == len(due) - 1).then_inc(S.mm, 1)

    g.vector.wait_ge(S.mm, 1 + len(due))
    g.vector.tensor_copy(T.ys[:], T.ps[:]).then_inc(S.cp, 1)
    g.sync.wait_ge(S.cp, 1)
    g.sync.dma_start(T.y[:], T.ys[:]).then_inc(S.st, 16)
    g.sync.wait_ge(S.st, 16)
    g.wait_ge(S.sent, sent)
